import numpy as np, ml_dtypes
CORES = [7,391,135,263,15,399,143,271]
N = 8
T, M = 1024, 1024
def entries(a): return a.T.reshape(-1)
def pack(v, P): return np.ascontiguousarray(np.asarray(v, np.int32).reshape(-1, P).T)
def lists(rng, how):
    I = rng.integers(0, T, (N, M))
    if how == "alike": I[:] = rng.integers(0, T, (N, 1))
    if how == "distinct": I = np.stack([rng.permutation(T)[:M] for r in range(N)])
    if how == "sorted": I = np.sort(I, axis=1)
    if how == "edge": I = np.where(rng.random((N, M)) < 0.5, 0, T - 1)
    return {"idx": np.stack([pack(I[r], 16) for r in range(N)])}
def setup_inputs(rng):
    return dict({"x": rng.standard_normal((N, 128, T), dtype=np.float32).astype(ml_dtypes.bfloat16)}, **lists(rng, "uniform"))
def setup_inputs_alike(rng):
    d = setup_inputs(rng); d.update(lists(rng, "alike"))
    for k in ("x",): d[k] = (d[k].astype(np.float32) * 1024.0).astype(d[k].dtype)
    return d
def setup_inputs_distinct(rng):
    d = setup_inputs(rng); d.update(lists(rng, "distinct"))
    for k in ("x",): d[k] = (d[k].astype(np.float32) * (1 / 1024.0)).astype(d[k].dtype)
    return d
def setup_inputs_edge(rng):
    d = setup_inputs(rng); d.update(lists(rng, "edge"))
    return d
def setup_inputs_sorted(rng):
    d = setup_inputs(rng); d.update(lists(rng, "sorted"))
    return d
def check_inputs(x):
    bad = []
    if x["idx"].min() < 0 or x["idx"].max() >= T: bad.append("idx out of range")
    return bad
def reference(x, idx):
    s = sum(x[r].astype(np.float64)[:, entries(idx[r])] for r in range(N)).astype(ml_dtypes.bfloat16)
    return {"y": np.broadcast_to(s, (N, 128, M))}

@@ -1,0 +1,149 @@
+from concourse.bass import DstId, RemoteDMATransfer
+from concourse.mybir import AluOpType, ActivationFunctionType
+
+COLS = 1024
+Q = COLS // 4
+H = Q // 2
+GRP = 16
+
+SCRATCH = {
+    "xs":    ("sbuf", [128, COLS], "bfloat16"),
+    "idx32": ("sbuf", [128, COLS // GRP], "int32"),
+    "idxf":  ("sbuf", [128, COLS // GRP], "float32"),
+    "rep":   ("sbuf", [128, 128], "float32"),
+    "ps":    ("psum", [128, COLS // GRP], "float32"),
+    "off":   ("sbuf", [128, COLS // GRP], "uint16"),
+    "gx":    ("sbuf", [128, COLS], "bfloat16"),
+    "rs":    ("sbuf", [128, 3 * Q], "bfloat16"),
+    "acc":   ("sbuf", [128, Q], "bfloat16"),
+    "cab":   ("sbuf", [128, Q], "bfloat16"),
+    "fin":   ("sbuf", [128, COLS], "bfloat16"),
+}
+SEMAPHORES = ["s_idx", "s_x", "s_one", "s_rep", "s_f", "s_mm", "s_off", "gq0", "gq1", "gq2", "gq3",
+              "rs0", "rs1", "rs2", "a1", "a2", "a3", "s_cab", "s_own", "ag0", "ag1", "ag2", "ag3", "sent", "s_y"]
+
+
+def _rack(topo, c):
+    return topo.rack(topo.host(c))
+
+
+def _peers(T, topo, c):
+    ranks = list(T.cores)
+    near = [o for o in ranks if o != c and _rack(topo, o) == _rack(topo, c)]
+    mate = [o for o in near if topo.mates(c, o)][0]
+    plane = [o for o in near if topo.same_plane(c, o)][0]
+    cross = [o for o in near if o != mate and o != plane][0]
+    cable = [o for o in ranks if _rack(topo, o) != _rack(topo, c) and topo.may_write(c, o)
+             and topo.chip(o) == topo.chip(c)][0]
+    return cross, plane, mate, cable
+
+
+def _quarter(T, topo, c):
+    ref = T.cores[0]
+    if _rack(topo, c) != _rack(topo, ref):
+        c = _peers(T, topo, c)[3]
+    if c == ref:
+        return 0
+    if topo.mates(c, ref):
+        return 1
+    if topo.same_plane(c, ref):
+        return 2
+    return 3
+
+
+def _engines(mask):
+    return bin(mask).count("1")
+
+
+def rank_program(g, core, T, topo):
+    if T.rank_of(core) is None:
+        return
+    S = T.sem
+    cross, plane, mate, cable = _peers(T, topo, core)
+    rackp = [cross, plane, mate]
+    own = _quarter(T, topo, core)
+    order = [_quarter(T, topo, o) for o in rackp] + [own]
+
+    def cols(q):
+        return slice(q * Q, (q + 1) * Q)
+
+    g.sync.dma_start(T.idx32[0:GRP, :], T.idx[:, :]).then_inc(S.s_idx, 16)
+    g.scalar.dma_start(T.xs[64:128, :], T.x[64:128, :]).then_inc(S.s_x, 16)
+    g.sync.dma_start(T.xs[0:64, :], T.x[0:64, :]).then_inc(S.s_x, 16)
+
+    g.vector.memset(T.rep[0:GRP, :], 1.0).then_inc(S.s_one, 1)
+    g.wait_ge(S.s_one, 1)
+    g.affine_select(T.rep[0:GRP, :], T.rep[0:GRP, :], [[0, 128 // GRP], [-1, GRP]], AluOpType.is_equal, 0.0, 0, 1
+                    ).then_inc(S.s_rep, 1)
+
+    g.vector.wait_ge(S.s_idx, 16)
+    g.vector.tensor_copy(T.idxf[0:GRP, :], T.idx32[0:GRP, :]).then_inc(S.s_f, 1)
+    g.tensor.wait_ge(S.s_rep, 1)
+    g.tensor.wait_ge(S.s_f, 1)
+    g.tensor.matmul(T.ps[:, :], T.rep[0:GRP, :], T.idxf[0:GRP, :], True, True).then_inc(S.s_mm, 1)
+    g.vector.wait_ge(S.s_mm, 1)
+    g.vector.tensor_copy(T.off[:, :], T.ps[:, :]).then_inc(S.s_off, 1)
+
+    g.vector.wait_ge(S.s_off, 1)
+    g.vector.wait_ge(S.s_x, 32)
+    g.scalar.wait_ge(S.s_off, 1)
+    g.scalar.wait_ge(S.s_x, 32)
+    for k, q in enumerate(order):
+        a = q * Q
+        g.vector.tensor_copy(T.gx[:, a:a + H],
+                             T.xs[:, 0:COLS].indirect(T.off[:, a // GRP:(a + H) // GRP])).then_inc(S["gq%d" % k], 1)
+        g.scalar.activation(T.gx[:, a + H:a + Q],
+                            T.xs[:, 0:COLS].indirect(T.off[:, (a + H) // GRP:(a + Q) // GRP]),
+                            ActivationFunctionType.Copy).then_inc(S["gq%d" % k], 1)
+
+    sent = 0
+    for k, o in enumerate(rackp):
+        rid, pid = topo.addr(o, core)
+        m = topo.mask(core, o)
+        g.wait_ge(S["gq%d" % k], 2)
+        g.remote_dma(T.rs[:, k * Q:(k + 1) * Q], T.gx[:, cols(order[k])], S["rs%d" % k], S.sent, pid, rid, m)
+        sent += _engines(m)
+
+    g.wait_ge(S.gq3, 2)
+    for k, o in enumerate(rackp):
+        g.wait_ge(S["rs%d" % k], _engines(topo.mask(o, core)))
+    rid, pid = topo.addr(cable, core)
+    m = topo.mask(core, cable)
+    g.remote_dma_fused([RemoteDMATransfer(
+        dst_ids=[DstId(rid=rid, pnc=pid)], dma_engine_mask=m, remote_sem=S.s_cab,
+        srcs=[T.gx[:, cols(own)]] + [T.rs[:, k * Q:(k + 1) * Q] for k in range(3)],
+        dsts=[T.cab[:, :]], alu_op=1)], local_sem=S.sent)
+    sent += _engines(m)
+
+    g.vector.wait_ge(S.gq3, 2)
+    g.vector.wait_ge(S.rs0, _engines(topo.mask(cross, core)))
+    g.vector.tensor_tensor(T.acc[:, :], T.gx[:, cols(own)], T.rs[:, 0:Q], AluOpType.add).then_inc(S.a1, 1)
+    g.vector.wait_ge(S.a1, 1)
+    g.vector.wait_ge(S.rs1, _engines(topo.mask(plane, core)))
+    g.vector.tensor_tensor(T.acc[:, :], T.acc[:, :], T.rs[:, Q:2 * Q], AluOpType.add).then_inc(S.a2, 1)
+    g.vector.wait_ge(S.a2, 1)
+    g.vector.wait_ge(S.rs2, _engines(topo.mask(mate, core)))
+    g.vector.tensor_tensor(T.acc[:, :], T.acc[:, :], T.rs[:, 2 * Q:3 * Q], AluOpType.add).then_inc(S.a3, 1)
+
+    ncab = _engines(topo.mask(cable, core))
+    g.wait_ge(S.a3, 1)
+    g.wait_ge(S.s_cab, ncab)
+    m = topo.mask(core, cross) & topo.mask(core, plane) & topo.mask(core, mate)
+    ids = [topo.addr(o, core) for o in rackp]
+    g.remote_dma_fused([RemoteDMATransfer(
+        dst_ids=[DstId(rid=rid, pnc=pid) for rid, pid in ids], dma_engine_mask=m, remote_sem=S["ag%d" % own],
+        srcs=[T.acc[:, :], T.cab[:, :]], dsts=[T.fin[:, cols(own)] for o in rackp], alu_op=1)], local_sem=S.sent)
+    sent += _engines(m)
+
+    g.vector.wait_ge(S.a3, 1)
+    g.vector.wait_ge(S.s_cab, ncab)
+    g.vector.tensor_tensor(T.fin[:, cols(own)], T.acc[:, :], T.cab[:, :], AluOpType.add).then_inc(S.s_own, 1)
+
+    g.sync.wait_ge(S.s_own, 1)
+    g.sync.dma_start(T.y[:, cols(own)], T.fin[:, cols(own)]).then_inc(S.s_y, 16)
+    for k, queue in ((0, g.scalar), (1, g.sync), (2, g.scalar)):
+        queue.wait_ge(S["ag%d" % order[k]], _engines(topo.mask(rackp[k], core)))
+        queue.dma_start(T.y[:, cols(order[k])], T.fin[:, cols(order[k])]).then_inc(S.s_y, 16)
+
+    g.wait_ge(S.sent, sent)
+    g.wait_ge(S.s_y, 64)

@@ -1,9 +1,10 @@
 from concourse.bass import DstId, RemoteDMATransfer
 from concourse.mybir import AluOpType, ActivationFunctionType
 
+WORLD = 512
 COLS = 1024
-Q = COLS // 4
-H = Q // 2
+P = COLS // 8
+HALF = COLS // 2
 GRP = 16
 
 SCRATCH = {
@@ -14,13 +15,17 @@ SCRATCH = {
     "ps":    ("psum", [128, COLS // GRP], "float32"),
     "off":   ("sbuf", [128, COLS // GRP], "uint16"),
     "gx":    ("sbuf", [128, COLS], "bfloat16"),
-    "rs":    ("sbuf", [128, 3 * Q], "bfloat16"),
-    "acc":   ("sbuf", [128, Q], "bfloat16"),
-    "cab":   ("sbuf", [128, Q], "bfloat16"),
+    "rs":    ("sbuf", [128, 4 * P], "bfloat16"),
+    "a1":    ("sbuf", [128, P], "bfloat16"),
+    "pacc":  ("psum", [128, P], "float32"),
+    "cab":   ("sbuf", [128, P], "bfloat16"),
     "fin":   ("sbuf", [128, COLS], "bfloat16"),
 }
-SEMAPHORES = ["s_idx", "s_x", "s_one", "s_rep", "s_f", "s_mm", "s_off", "gq0", "gq1", "gq2", "gq3",
-              "rs0", "rs1", "rs2", "a1", "a2", "a3", "s_cab", "s_own", "ag0", "ag1", "ag2", "ag3", "sent", "s_y"]
+SEMAPHORES = ["s_idx", "s_x", "s_one", "s_rep", "s_f", "s_mm", "s_off"] + ["gq%d" % k for k in range(8)] + [
+    "rs0", "rs1", "rs2", "rs3", "a1", "a2", "a3", "s_cab", "s_own", "agh", "agr0", "agr1", "agr2", "agr3",
+    "sent", "s_y"]
+
+_CACHE = {}
 
 
 def _rack(topo, c):
@@ -51,21 +56,104 @@ def _quarter(T, topo, c):
     return 3
 
 
+def _helpers(T, topo):
+    if "h" not in _CACHE:
+        h = {}
+        for c in T.cores:
+            near = [o for o in T.cores if _rack(topo, o) == _rack(topo, c)]
+            cand = [o for o in range(WORLD)
+                    if topo.host(o) == topo.host(c) and topo.chip(o) == topo.chip(c) and o != c
+                    and topo.die(o) != topo.die(c) and all(topo.may_write(o, r) for r in near)]
+            h[c] = cand[-1]
+        _CACHE["h"] = h
+    return _CACHE["h"]
+
+
 def _engines(mask):
     return bin(mask).count("1")
 
 
+def _slot(T, k):
+    return T.rs[:, k * P:(k + 1) * P]
+
+
+def _owner(g, core, T, topo, early, early_waits, n_plane, n_mate, partner, piece, spread):
+    S, V = T.sem, g.vector
+    add = AluOpType.add
+    sent = 0
+    for sem, n in early_waits:
+        V.wait_ge(sem, n)
+    V.tensor_tensor(T.a1[:, :], early[0], early[1], add).then_inc(S.a1, 1)
+
+    g.wait_ge(S.a1, 1)
+    g.wait_ge(S.rs1, n_plane)
+    g.wait_ge(S.rs2, n_mate)
+    rid, pid = topo.addr(partner, core)
+    m = topo.mask(core, partner)
+    g.remote_dma_fused([RemoteDMATransfer(
+        dst_ids=[DstId(rid=rid, pnc=pid)], dma_engine_mask=m, remote_sem=S.s_cab,
+        srcs=[T.a1[:, :], _slot(T, 1), _slot(T, 2)], dsts=[T.cab[:, :]], alu_op=1)], local_sem=S.sent)
+    sent += _engines(m)
+
+    V.wait_ge(S.a1, 1)
+    V.wait_ge(S.rs1, n_plane)
+    V.tensor_tensor(T.pacc[:, :], T.a1[:, :], _slot(T, 1), add).then_inc(S.a2, 1)
+    V.wait_ge(S.a2, 1)
+    V.wait_ge(S.rs2, n_mate)
+    V.tensor_tensor(T.pacc[:, :], T.pacc[:, :], _slot(T, 2), add).then_inc(S.a3, 1)
+    V.wait_ge(S.a3, 1)
+    V.wait_ge(S.s_cab, _engines(topo.mask(partner, core)))
+    V.tensor_tensor(T.fin[:, piece], T.pacc[:, :], T.cab[:, :], add).then_inc(S.s_own, 1)
+
+    g.wait_ge(S.s_own, 1)
+    for dests, m, sem in spread:
+        ids = [topo.addr(o, core) for o in dests]
+        g.remote_dma_fused([RemoteDMATransfer(
+            dst_ids=[DstId(rid=rid, pnc=pid) for rid, pid in ids], dma_engine_mask=m, remote_sem=sem,
+            srcs=[T.fin[:, piece]], dsts=[T.fin[:, piece] for o in dests], alu_op=0)], local_sem=S.sent)
+        sent += _engines(m)
+    return sent
+
+
+def _helper_program(g, core, T, topo, rank):
+    S = T.sem
+    helpers = _helpers(T, topo)
+    cross, plane, mate, cable = _peers(T, topo, rank)
+    q = _quarter(T, topo, rank)
+    piece = slice(q * P, (q + 1) * P)
+    away = topo.mask(core, cross) & topo.mask(core, plane) & topo.mask(core, mate)
+    home = topo.mask(core, rank) & ~away
+    n_home = _engines(topo.mask(rank, core) & ~topo.mask(rank, helpers[plane]))
+    sent = _owner(g, core, T, topo,
+                  (_slot(T, 0), _slot(T, 3)),
+                  [(S.rs0, _engines(topo.mask(cross, core))), (S.rs3, n_home)],
+                  _engines(topo.mask(plane, core)), _engines(topo.mask(mate, core)),
+                  helpers[cable], piece,
+                  [([cross, plane, mate], away, S.agh), ([rank], home, S.agh)])
+    g.wait_ge(S.sent, sent)
+
+
 def rank_program(g, core, T, topo):
+    helpers = _helpers(T, topo)
     if T.rank_of(core) is None:
+        for r in T.cores:
+            if helpers[r] == core:
+                _helper_program(g, core, T, topo, r)
         return
     S = T.sem
     cross, plane, mate, cable = _peers(T, topo, core)
     rackp = [cross, plane, mate]
     own = _quarter(T, topo, core)
-    order = [_quarter(T, topo, o) for o in rackp] + [own]
+    qs = [_quarter(T, topo, o) for o in rackp]
+    mine = helpers[core]
 
-    def cols(q):
-        return slice(q * Q, (q + 1) * Q)
+    def hcol(q):
+        return slice(q * P, (q + 1) * P)
+
+    def rcol(q):
+        return slice(HALF + q * P, HALF + (q + 1) * P)
+
+    order = [hcol(qs[0]), hcol(qs[1]), hcol(own), hcol(qs[2]), rcol(qs[0]), rcol(qs[1]), rcol(qs[2]), rcol(own)]
 
     g.sync.dma_start(T.idx32[0:GRP, :], T.idx[:, :]).then_inc(S.s_idx, 16)
     g.scalar.dma_start(T.xs[64:128, :], T.x[64:128, :]).then_inc(S.s_x, 16)
@@ -88,62 +176,62 @@ def rank_program(g, core, T, topo):
     g.vector.wait_ge(S.s_x, 32)
     g.scalar.wait_ge(S.s_off, 1)
     g.scalar.wait_ge(S.s_x, 32)
-    for k, q in enumerate(order):
-        a = q * Q
-        g.vector.tensor_copy(T.gx[:, a:a + H],
-                             T.xs[:, 0:COLS].indirect(T.off[:, a // GRP:(a + H) // GRP])).then_inc(S["gq%d" % k], 1)
-        g.scalar.activation(T.gx[:, a + H:a + Q],
-                            T.xs[:, 0:COLS].indirect(T.off[:, (a + H) // GRP:(a + Q) // GRP]),
+    for k, sl in enumerate(order):
+        a, h, b = sl.start, sl.start + P // 2, sl.stop
+        g.vector.tensor_copy(T.gx[:, a:h],
+                             T.xs[:, 0:COLS].indirect(T.off[:, a // GRP:h // GRP])).then_inc(S["gq%d" % k], 1)
+        g.scalar.activation(T.gx[:, h:b], T.xs[:, 0:COLS].indirect(T.off[:, h // GRP:b // GRP]),
                             ActivationFunctionType.Copy).then_inc(S["gq%d" % k], 1)
 
     sent = 0
-    for k, o in enumerate(rackp):
-        rid, pid = topo.addr(o, core)
-        m = topo.mask(core, o)
-        g.wait_ge(S["gq%d" % k], 2)
-        g.remote_dma(T.rs[:, k * Q:(k + 1) * Q], T.gx[:, cols(order[k])], S["rs%d" % k], S.sent, pid, rid, m)
-        sent += _engines(m)
 
+    def send(dst, k, sl):
+        rid, pid = topo.addr(dst, core)
+        m = topo.mask(core, dst)
+        g.remote_dma(_slot(T, k), T.gx[:, sl], S["rs%d" % k], S.sent, pid, rid, m)
+        return _engines(m)
+
+    g.wait_ge(S.gq0, 2)
+    sent += send(helpers[cross], 0, order[0])
+    g.wait_ge(S.gq1, 2)
+    g.wait_ge(S.gq2, 2)
+    m_away = topo.mask(core, helpers[plane])
+    m_home = topo.mask(core, mine) & ~m_away
+    rid_a, pid_a = topo.addr(helpers[plane], core)
+    rid_h, pid_h = topo.addr(mine, core)
+    g.remote_dma_fused([
+        RemoteDMATransfer(dst_ids=[DstId(rid=rid_a, pnc=pid_a)], dma_engine_mask=m_away, remote_sem=S.rs1,
+                          srcs=[T.gx[:, order[1]]], dsts=[_slot(T, 1)], alu_op=0),
+        RemoteDMATransfer(dst_ids=[DstId(rid=rid_h, pnc=pid_h)], dma_engine_mask=m_home, remote_sem=S.rs3,
+                          srcs=[T.gx[:, order[2]]], dsts=[_slot(T, 3)], alu_op=0)], local_sem=S.sent)
+    sent += _engines(m_away) + _engines(m_home)
     g.wait_ge(S.gq3, 2)
+    sent += send(helpers[mate], 2, order[3])
     for k, o in enumerate(rackp):
-        g.wait_ge(S["rs%d" % k], _engines(topo.mask(o, core)))
-    rid, pid = topo.addr(cable, core)
-    m = topo.mask(core, cable)
-    g.remote_dma_fused([RemoteDMATransfer(
-        dst_ids=[DstId(rid=rid, pnc=pid)], dma_engine_mask=m, remote_sem=S.s_cab,
-        srcs=[T.gx[:, cols(own)]] + [T.rs[:, k * Q:(k + 1) * Q] for k in range(3)],
-        dsts=[T.cab[:, :]], alu_op=1)], local_sem=S.sent)
-    sent += _engines(m)
+        g.wait_ge(S["gq%d" % (4 + k)], 2)
+        sent += send(o, k, order[4 + k])
 
-    g.vector.wait_ge(S.gq3, 2)
-    g.vector.wait_ge(S.rs0, _engines(topo.mask(cross, core)))
-    g.vector.tensor_tensor(T.acc[:, :], T.gx[:, cols(own)], T.rs[:, 0:Q], AluOpType.add).then_inc(S.a1, 1)
-    g.vector.wait_ge(S.a1, 1)
-    g.vector.wait_ge(S.rs1, _engines(topo.mask(plane, core)))
-    g.vector.tensor_tensor(T.acc[:, :], T.acc[:, :], T.rs[:, Q:2 * Q], AluOpType.add).then_inc(S.a2, 1)
-    g.vector.wait_ge(S.a2, 1)
-    g.vector.wait_ge(S.rs2, _engines(topo.mask(mate, core)))
-    g.vector.tensor_tensor(T.acc[:, :], T.acc[:, :], T.rs[:, 2 * Q:3 * Q], AluOpType.add).then_inc(S.a3, 1)
+    away = topo.mask(core, cross) & topo.mask(core, plane) & topo.mask(core, mate)
+    sent += _owner(g, core, T, topo,
+                   (T.gx[:, rcol(own)], _slot(T, 0)),
+                   [(S.gq7, 2), (S.rs0, _engines(topo.mask(cross, core)))],
+                   _engines(topo.mask(plane, core)), _engines(topo.mask(mate, core)),
+                   cable, rcol(own),
+                   [(rackp, away, S["agr%d" % own])])
 
-    ncab = _engines(topo.mask(cable, core))
-    g.wait_ge(S.a3, 1)
-    g.wait_ge(S.s_cab, ncab)
-    m = topo.mask(core, cross) & topo.mask(core, plane) & topo.mask(core, mate)
-    ids = [topo.addr(o, core) for o in rackp]
-    g.remote_dma_fused([RemoteDMATransfer(
-        dst_ids=[DstId(rid=rid, pnc=pid) for rid, pid in ids], dma_engine_mask=m, remote_sem=S["ag%d" % own],
-        srcs=[T.acc[:, :], T.cab[:, :]], dsts=[T.fin[:, cols(own)] for o in rackp], alu_op=1)], local_sem=S.sent)
-    sent += _engines(m)
-
-    g.vector.wait_ge(S.a3, 1)
-    g.vector.wait_ge(S.s_cab, ncab)
-    g.vector.tensor_tensor(T.fin[:, cols(own)], T.acc[:, :], T.cab[:, :], AluOpType.add).then_inc(S.s_own, 1)
-
-    g.sync.wait_ge(S.s_own, 1)
-    g.sync.dma_start(T.y[:, cols(own)], T.fin[:, cols(own)]).then_inc(S.s_y, 16)
+    n_h = 0
+    for o in rackp:
+        ho = helpers[o]
+        n_h += _engines(topo.mask(ho, core) & topo.mask(ho, _peers(T, topo, o)[0]) & topo.mask(ho, _peers(T, topo, o)[1])
+                        & topo.mask(ho, _peers(T, topo, o)[2]))
+    n_h += _engines(topo.mask(mine, core) & ~topo.mask(mine, cross))
+    g.sync.wait_ge(S.agh, n_h)
+    g.sync.dma_start(T.y[:, 0:HALF], T.fin[:, 0:HALF]).then_inc(S.s_y, 16)
+    g.scalar.wait_ge(S.s_own, 1)
+    g.scalar.dma_start(T.y[:, rcol(own)], T.fin[:, rcol(own)]).then_inc(S.s_y, 16)
     for k, queue in ((0, g.scalar), (1, g.sync), (2, g.scalar)):
-        queue.wait_ge(S["ag%d" % order[k]], _engines(topo.mask(rackp[k], core)))
-        queue.dma_start(T.y[:, cols(order[k])], T.fin[:, cols(order[k])]).then_inc(S.s_y, 16)
+        queue.wait_ge(S["agr%d" % qs[k]], _engines(topo.mask(rackp[k], core)))
+        queue.dma_start(T.y[:, rcol(qs[k])], T.fin[:, rcol(qs[k])]).then_inc(S.s_y, 16)
 
     g.wait_ge(S.sent, sent)
-    g.wait_ge(S.s_y, 64)
+    g.wait_ge(S.s_y, 16 * 5)

from concourse.bass import DstId, RemoteDMATransfer
from concourse.mybir import AluOpType, ActivationFunctionType

WORLD = 512
COLS = 1024
P = COLS // 8
HALF = COLS // 2
GRP = 16

SCRATCH = {
    "xs":    ("sbuf", [128, COLS], "bfloat16"),
    "idx32": ("sbuf", [128, COLS // GRP], "int32"),
    "idxf":  ("sbuf", [128, COLS // GRP], "float32"),
    "rep":   ("sbuf", [128, 128], "float32"),
    "ps":    ("psum", [128, COLS // GRP], "float32"),
    "off":   ("sbuf", [128, COLS // GRP], "uint16"),
    "gx":    ("sbuf", [128, COLS], "bfloat16"),
    "rs":    ("sbuf", [128, 4 * P], "bfloat16"),
    "a1":    ("sbuf", [128, P], "bfloat16"),
    "pacc":  ("psum", [128, P], "float32"),
    "cab":   ("sbuf", [128, P], "bfloat16"),
    "fin":   ("sbuf", [128, COLS], "bfloat16"),
}
SEMAPHORES = ["s_idx", "s_x", "s_one", "s_rep", "s_f", "s_mm", "s_off"] + ["gq%d" % k for k in range(8)] + [
    "rs0", "rs1", "rs2", "rs3", "a1", "a2", "a3", "s_cab", "s_own", "agh", "agr0", "agr1", "agr2", "agr3",
    "sent", "s_y"]

_CACHE = {}


def _rack(topo, c):
    return topo.rack(topo.host(c))


def _peers(T, topo, c):
    ranks = list(T.cores)
    near = [o for o in ranks if o != c and _rack(topo, o) == _rack(topo, c)]
    mate = [o for o in near if topo.mates(c, o)][0]
    plane = [o for o in near if topo.same_plane(c, o)][0]
    cross = [o for o in near if o != mate and o != plane][0]
    cable = [o for o in ranks if _rack(topo, o) != _rack(topo, c) and topo.may_write(c, o)
             and topo.chip(o) == topo.chip(c)][0]
    return cross, plane, mate, cable


def _quarter(T, topo, c):
    ref = T.cores[0]
    if _rack(topo, c) != _rack(topo, ref):
        c = _peers(T, topo, c)[3]
    if c == ref:
        return 0
    if topo.mates(c, ref):
        return 1
    if topo.same_plane(c, ref):
        return 2
    return 3


def _helpers(T, topo):
    if "h" not in _CACHE:
        h = {}
        for c in T.cores:
            near = [o for o in T.cores if _rack(topo, o) == _rack(topo, c)]
            cand = [o for o in range(WORLD)
                    if topo.host(o) == topo.host(c) and topo.chip(o) == topo.chip(c) and o != c
                    and topo.die(o) != topo.die(c) and all(topo.may_write(o, r) for r in near)]
            h[c] = cand[-1]
        _CACHE["h"] = h
    return _CACHE["h"]


def _engines(mask):
    return bin(mask).count("1")


def _slot(T, k):
    return T.rs[:, k * P:(k + 1) * P]


def _owner(g, core, T, topo, early, early_waits, n_plane, n_mate, partner, piece, spread):
    S, V = T.sem, g.vector
    add = AluOpType.add
    sent = 0
    for sem, n in early_waits:
        V.wait_ge(sem, n)
    V.tensor_tensor(T.a1[:, :], early[0], early[1], add).then_inc(S.a1, 1)

    g.wait_ge(S.a1, 1)
    g.wait_ge(S.rs1, n_plane)
    g.wait_ge(S.rs2, n_mate)
    rid, pid = topo.addr(partner, core)
    m = topo.mask(core, partner)
    g.remote_dma_fused([RemoteDMATransfer(
        dst_ids=[DstId(rid=rid, pnc=pid)], dma_engine_mask=m, remote_sem=S.s_cab,
        srcs=[T.a1[:, :], _slot(T, 1), _slot(T, 2)], dsts=[T.cab[:, :]], alu_op=1)], local_sem=S.sent)
    sent += _engines(m)

    V.wait_ge(S.a1, 1)
    V.wait_ge(S.rs1, n_plane)
    V.tensor_tensor(T.pacc[:, :], T.a1[:, :], _slot(T, 1), add).then_inc(S.a2, 1)
    V.wait_ge(S.a2, 1)
    V.wait_ge(S.rs2, n_mate)
    V.tensor_tensor(T.pacc[:, :], T.pacc[:, :], _slot(T, 2), add).then_inc(S.a3, 1)
    V.wait_ge(S.a3, 1)
    V.wait_ge(S.s_cab, _engines(topo.mask(partner, core)))
    V.tensor_tensor(T.fin[:, piece], T.pacc[:, :], T.cab[:, :], add).then_inc(S.s_own, 1)

    g.wait_ge(S.s_own, 1)
    for dests, m, sem in spread:
        ids = [topo.addr(o, core) for o in dests]
        g.remote_dma_fused([RemoteDMATransfer(
            dst_ids=[DstId(rid=rid, pnc=pid) for rid, pid in ids], dma_engine_mask=m, remote_sem=sem,
            srcs=[T.fin[:, piece]], dsts=[T.fin[:, piece] for o in dests], alu_op=0)], local_sem=S.sent)
        sent += _engines(m)
    return sent


def _helper_program(g, core, T, topo, rank):
    S = T.sem
    helpers = _helpers(T, topo)
    cross, plane, mate, cable = _peers(T, topo, rank)
    q = _quarter(T, topo, rank)
    piece = slice(q * P, (q + 1) * P)
    away = topo.mask(core, cross) & topo.mask(core, plane) & topo.mask(core, mate)
    home = topo.mask(core, rank) & ~away
    n_home = _engines(topo.mask(rank, core) & ~topo.mask(rank, helpers[plane]))
    sent = _owner(g, core, T, topo,
                  (_slot(T, 0), _slot(T, 3)),
                  [(S.rs0, _engines(topo.mask(cross, core))), (S.rs3, n_home)],
                  _engines(topo.mask(plane, core)), _engines(topo.mask(mate, core)),
                  helpers[cable], piece,
                  [([cross, plane, mate], away, S.agh), ([rank], home, S.agh)])
    g.wait_ge(S.sent, sent)


def rank_program(g, core, T, topo):
    helpers = _helpers(T, topo)
    if T.rank_of(core) is None:
        for r in T.cores:
            if helpers[r] == core:
                _helper_program(g, core, T, topo, r)
        return
    S = T.sem
    cross, plane, mate, cable = _peers(T, topo, core)
    rackp = [cross, plane, mate]
    own = _quarter(T, topo, core)
    qs = [_quarter(T, topo, o) for o in rackp]
    mine = helpers[core]

    def hcol(q):
        return slice(q * P, (q + 1) * P)

    def rcol(q):
        return slice(HALF + q * P, HALF + (q + 1) * P)

    order = [hcol(qs[0]), hcol(qs[1]), hcol(own), hcol(qs[2]), rcol(qs[0]), rcol(qs[1]), rcol(qs[2]), rcol(own)]

    g.sync.dma_start(T.idx32[0:GRP, :], T.idx[:, :]).then_inc(S.s_idx, 16)
    g.scalar.dma_start(T.xs[64:128, :], T.x[64:128, :]).then_inc(S.s_x, 16)
    g.sync.dma_start(T.xs[0:64, :], T.x[0:64, :]).then_inc(S.s_x, 16)

    g.vector.memset(T.rep[0:GRP, :], 1.0).then_inc(S.s_one, 1)
    g.wait_ge(S.s_one, 1)
    g.affine_select(T.rep[0:GRP, :], T.rep[0:GRP, :], [[0, 128 // GRP], [-1, GRP]], AluOpType.is_equal, 0.0, 0, 1
                    ).then_inc(S.s_rep, 1)

    g.vector.wait_ge(S.s_idx, 16)
    g.vector.tensor_copy(T.idxf[0:GRP, :], T.idx32[0:GRP, :]).then_inc(S.s_f, 1)
    g.tensor.wait_ge(S.s_rep, 1)
    g.tensor.wait_ge(S.s_f, 1)
    g.tensor.matmul(T.ps[:, :], T.rep[0:GRP, :], T.idxf[0:GRP, :], True, True).then_inc(S.s_mm, 1)
    g.vector.wait_ge(S.s_mm, 1)
    g.vector.tensor_copy(T.off[:, :], T.ps[:, :]).then_inc(S.s_off, 1)

    g.vector.wait_ge(S.s_off, 1)
    g.vector.wait_ge(S.s_x, 32)
    g.scalar.wait_ge(S.s_off, 1)
    g.scalar.wait_ge(S.s_x, 32)
    for k, sl in enumerate(order):
        a, h, b = sl.start, sl.start + P // 2, sl.stop
        g.vector.tensor_copy(T.gx[:, a:h],
                             T.xs[:, 0:COLS].indirect(T.off[:, a // GRP:h // GRP])).then_inc(S["gq%d" % k], 1)
        g.scalar.activation(T.gx[:, h:b], T.xs[:, 0:COLS].indirect(T.off[:, h // GRP:b // GRP]),
                            ActivationFunctionType.Copy).then_inc(S["gq%d" % k], 1)

    sent = 0

    def send(dst, k, sl):
        rid, pid = topo.addr(dst, core)
        m = topo.mask(core, dst)
        g.remote_dma(_slot(T, k), T.gx[:, sl], S["rs%d" % k], S.sent, pid, rid, m)
        return _engines(m)

    g.wait_ge(S.gq0, 2)
    sent += send(helpers[cross], 0, order[0])
    g.wait_ge(S.gq1, 2)
    g.wait_ge(S.gq2, 2)
    m_away = topo.mask(core, helpers[plane])
    m_home = topo.mask(core, mine) & ~m_away
    rid_a, pid_a = topo.addr(helpers[plane], core)
    rid_h, pid_h = topo.addr(mine, core)
    g.remote_dma_fused([
        RemoteDMATransfer(dst_ids=[DstId(rid=rid_a, pnc=pid_a)], dma_engine_mask=m_away, remote_sem=S.rs1,
                          srcs=[T.gx[:, order[1]]], dsts=[_slot(T, 1)], alu_op=0),
        RemoteDMATransfer(dst_ids=[DstId(rid=rid_h, pnc=pid_h)], dma_engine_mask=m_home, remote_sem=S.rs3,
                          srcs=[T.gx[:, order[2]]], dsts=[_slot(T, 3)], alu_op=0)], local_sem=S.sent)
    sent += _engines(m_away) + _engines(m_home)
    g.wait_ge(S.gq3, 2)
    sent += send(helpers[mate], 2, order[3])
    for k, o in enumerate(rackp):
        g.wait_ge(S["gq%d" % (4 + k)], 2)
        sent += send(o, k, order[4 + k])

    away = topo.mask(core, cross) & topo.mask(core, plane) & topo.mask(core, mate)
    sent += _owner(g, core, T, topo,
                   (T.gx[:, rcol(own)], _slot(T, 0)),
                   [(S.gq7, 2), (S.rs0, _engines(topo.mask(cross, core)))],
                   _engines(topo.mask(plane, core)), _engines(topo.mask(mate, core)),
                   cable, rcol(own),
                   [(rackp, away, S["agr%d" % own])])

    n_h = 0
    for o in rackp:
        ho = helpers[o]
        n_h += _engines(topo.mask(ho, core) & topo.mask(ho, _peers(T, topo, o)[0]) & topo.mask(ho, _peers(T, topo, o)[1])
                        & topo.mask(ho, _peers(T, topo, o)[2]))
    n_h += _engines(topo.mask(mine, core) & ~topo.mask(mine, cross))
    g.sync.wait_ge(S.agh, n_h)
    g.sync.dma_start(T.y[:, 0:HALF], T.fin[:, 0:HALF]).then_inc(S.s_y, 16)
    g.scalar.wait_ge(S.s_own, 1)
    g.scalar.dma_start(T.y[:, rcol(own)], T.fin[:, rcol(own)]).then_inc(S.s_y, 16)
    for k, queue in ((0, g.scalar), (1, g.sync), (2, g.scalar)):
        queue.wait_ge(S["agr%d" % qs[k]], _engines(topo.mask(rackp[k], core)))
        queue.dma_start(T.y[:, rcol(qs[k])], T.fin[:, rcol(qs[k])]).then_inc(S.s_y, 16)

    g.wait_ge(S.sent, sent)
    g.wait_ge(S.s_y, 16 * 5)
